import numpy as np, ml_dtypes
CORES = [22,46,70,150,174,198,278,302,326,406,430,454]
N = 12
VB, TK = 4, 128
def setup_inputs(rng):
    h = rng.standard_normal((128, TK), dtype=np.float32) / 4; w = rng.standard_normal((N, 128, VB * 128), dtype=np.float32)
    a = 2 * np.pi * rng.random((TK)); s = 400 * rng.random((TK)) ** 1.5; h[0] = s * np.cos(a); h[1] = s * np.sin(a); h[2] = 150 * rng.standard_normal((TK)); w[:, 2, :] = 1 + w[:, 2, :] / 50
    a = (2 * np.pi * rng.random() + np.pi / 2 * (rng.permutation(N).reshape(N, 1, 1) + 0.5) / N - 0.5 + (np.arange(VB).reshape(1, VB, 1) + rng.random((N, VB, 128))) / VB).reshape(N, VB * 128); w[:, 0, :] = np.cos(a); w[:, 1, :] = np.sin(a)
    tgt = rng.integers(0, N * VB * 128, size=TK)
    oh = np.zeros((N * VB * 128, TK), np.float32); oh[tgt, np.arange(TK)] = 1.0
    oh = oh.reshape(N, VB, 128, TK).transpose(0, 2, 1, 3).reshape(N, 128, VB * TK)
    return {"h": np.broadcast_to(h, (N, 128, TK)).astype(ml_dtypes.bfloat16), "w": w.astype(ml_dtypes.bfloat16), "oh": oh.astype(ml_dtypes.bfloat16)}
def reference(h, w, oh):
    H, W, OH = h.astype(np.float64), w.astype(np.float64), oh.astype(np.float64)
    Z = np.concatenate([W[r].T @ H[r] for r in range(N)], axis=0)
    O = np.concatenate([OH[r][:, TK * b:TK * b + TK] for r in range(N) for b in range(VB)], axis=0)
    m = Z.max(axis=0)
    l = m + np.log(np.exp(Z - m).sum(axis=0)) - (O * Z).sum(axis=0)
    return {"l": np.broadcast_to(l.astype(np.float32), (N, 1, TK))}

@@ -1,0 +1,169 @@
+from concourse.bass import DstId, RemoteDMATransfer
+from concourse.mybir import AluOpType, AxisListType, ActivationFunctionType
+
+N = 12
+W1 = 64
+W2 = 512 - W1
+
+SCRATCH = {
+    "hsb": ("sbuf", [128, 128], "bfloat16"),
+    "wsb": ("sbuf", [128, 512], "bfloat16"),
+    "ohsb": ("sbuf", [128, 512], "bfloat16"),
+    "junk": ("sbuf", [128, 512], "float32"),
+    "prod": ("sbuf", [128, 512], "float32"),
+    "ones": ("sbuf", [128, 4], "float32"),
+    "st": ("sbuf", [128, 8], "float32"),
+    "sel": ("sbuf", [128, 52], "float32"),
+    "gat": ("sbuf", [128, 128], "float32"),
+    "tl": ("sbuf", [128, 32], "float32"),
+    "land": ("dram", [N, 128, 4], "float32"),
+    "zA1": ("psum", [128, 512], "float32"),
+    "zA2": ("psum", [128, 512], "float32"),
+    "zv": ("psum", [128, 512], "float32"),
+    "tgp": ("psum", [128, 512], "float32"),
+    "fin": ("psum", [128, 512], "float32"),
+    "fin2": ("psum", [128, 512], "float32"),
+}
+SEMAPHORES = ["ld_h", "ld_w1", "ld_w2", "ld_oh", "c_ones", "c_sel", "selA", "selB", "selC",
+              "mA1", "mA2", "mB", "vA", "vB", "vC", "vp0", "vp1", "vp2", "vp3", "mT", "vT",
+              "aE1", "aE", "aE2", "vS", "packed", "peer_in", "arrived", "sent", "unp",
+              "pf", "pf2", "t1", "t2", "t3", "t4", "t5", "t6", "t7", "stored"]
+
+ADD, MUL, SUB = AluOpType.add, AluOpType.mult, AluOpType.subtract
+MAX, MIN = AluOpType.max, AluOpType.min
+X = AxisListType.X
+EXP, LN, IDENT = ActivationFunctionType.Exp, ActivationFunctionType.Ln, ActivationFunctionType.Identity
+
+
+def _engines(topo, src, dsts):
+    m = topo.mask(src, dsts[0])
+    for d in dsts[1:]:
+        m &= topo.mask(src, d)
+    return [1 << i for i in range(16) if (m >> i) & 1]
+
+
+def rank_program(g, core, T, topo):
+    rank = T.rank_of(core)
+    if rank is None:
+        return
+    S = T.sem
+    te, ve, sc, sy = g.tensor, g.vector, g.scalar, g.sync
+
+    my_rack = topo.rack(topo.host(core))
+    others = [c for c in T.cores if c != core]
+    mates = [c for c in others if topo.rack(topo.host(c)) == my_rack]
+    peer = [c for c in others if topo.rack(topo.host(c)) != my_rack
+            and topo.may_write(core, c) and topo.chip(c) == topo.chip(core)][0]
+    peer_rank = T.rank_of(peer)
+    eng = _engines(topo, core, mates + [peer])
+
+    sc.dma_start(T.hsb[:], T.h[:]).then_inc(S.ld_h, 16)
+    sy.dma_start(T.wsb[:, 0:W1], T.w[:, 0:W1]).then_inc(S.ld_w1, 16)
+    sc.dma_start(T.wsb[:, W1:512], T.w[:, W1:512]).then_inc(S.ld_w2, 16)
+    sy.dma_start(T.ohsb[:], T.oh[:]).then_inc(S.ld_oh, 16)
+
+    ve.memset(T.sel[0:48, 0:48], 1.0).then_inc(S.c_sel, 1)
+    ve.memset(T.ones[:, 0:1], 1.0).then_inc(S.c_ones, 1)
+    g.wait_ge(S.c_sel, 1)
+    g.affine_select(T.sel[0:48, 0:48], T.sel[0:48, 0:48], [[-1, 4], [-4, 12]], AluOpType.is_equal, 0.0, 0, 1).then_inc(S.selA, 1)
+    ve.wait_ge(S.selA, 1)
+    ve.tensor_reduce(out=T.sel[0:48, 48:49], in_=T.sel[0:48, 36:48], axis=X, op=ADD).then_inc(S.selB, 1)
+    ve.tensor_tensor(T.sel[0:48, 12:24], T.sel[0:48, 12:24], T.sel[0:48, 24:36], ADD).then_inc(S.selC, 1)
+
+    te.wait_ge(S.ld_h, 16)
+    te.wait_ge(S.ld_w1, 16)
+    te.matmul(T.zA1[:, 0:W1], T.hsb[:], T.wsb[:, 0:W1], start=True, stop=True).then_inc(S.mA1, 1)
+    te.wait_ge(S.ld_w2, 16)
+    te.matmul(T.zA2[:, 0:W2], T.hsb[:], T.wsb[:, W1:512], start=True, stop=True).then_inc(S.mA2, 1)
+    for b in range(4):
+        te.matmul(T.zv[:, 128 * b:128 * b + 128], T.wsb[:, 128 * b:128 * b + 128], T.hsb[:],
+                  start=True, stop=True).then_inc(S.mB, 1)
+
+    ve.wait_ge(S.mA1, 1)
+    ve.tensor_reduce(out=T.st[:, 0:1], in_=T.zA1[:, 0:W1], axis=X, op=MAX, negate=True).then_inc(S.vA, 1)
+    ve.wait_ge(S.mA2, 1)
+    ve.tensor_reduce(out=T.st[:, 1:2], in_=T.zA2[:, 0:W2], axis=X, op=MAX, negate=True).then_inc(S.vB, 1)
+    ve.wait_ge(S.vA, 1)
+    ve.wait_ge(S.vB, 1)
+    ve.tensor_tensor(T.st[:, 2:3], T.st[:, 0:1], T.st[:, 1:2], MIN).then_inc(S.vC, 1)
+    ve.wait_ge(S.mB, 4)
+    ve.wait_ge(S.ld_oh, 16)
+    for b in range(4):
+        blk = slice(128 * b, 128 * b + 128)
+        ve.tensor_tensor(T.prod[:, blk], T.zv[:, blk], T.ohsb[:, blk], MUL).then_inc(S["vp%d" % b], 1)
+
+    sc.wait_ge(S.vA, 1)
+    sc.activation(T.junk[:, 0:W1], T.zA1[:, 0:W1], EXP, bias=T.st[:, 0:1], scale=1.0,
+                  accum_out=T.st[:, 3:4]).then_inc(S.aE1, 1)
+    sc.wait_ge(S.vC, 1)
+    sc.activation(T.st[:, 5:6], T.st[:, 0:1], EXP, bias=T.st[:, 2:3], scale=-1.0).then_inc(S.aE, 1)
+    sc.activation(T.junk[:, W1:512], T.zA2[:, 0:W2], EXP, bias=T.st[:, 2:3], scale=1.0,
+                  accum_out=T.st[:, 4:5]).then_inc(S.aE2, 1)
+
+    te.wait_ge(S.c_ones, 1)
+    for b in range(4):
+        te.wait_ge(S["vp%d" % b], 1)
+        te.matmul(T.tgp[:, 0:1], T.prod[:, 128 * b:128 * b + 128], T.ones[:, 0:1],
+                  start=(b == 0), stop=(b == 3)).then_inc(S.mT, 1)
+    ve.wait_ge(S.aE1, 1)
+    ve.wait_ge(S.aE, 1)
+    ve.tensor_tensor(T.st[:, 6:7], T.st[:, 3:4], T.st[:, 5:6], MUL).then_inc(S.vS, 1)
+    ve.wait_ge(S.mT, 4)
+    ve.tensor_copy(T.st[:, 7:8], T.tgp[:, 0:1]).then_inc(S.vT, 1)
+
+    sy.wait_ge(S.vC, 1)
+    sy.dma_start(T.land[rank, 0:32, :], T.st[:, 2:3]).then_inc(S.packed, 16)
+    sy.wait_ge(S.vS, 1)
+    sy.dma_start(T.land[rank, 32:64, :], T.st[:, 6:7]).then_inc(S.packed, 16)
+    sy.wait_ge(S.vT, 1)
+    sy.dma_start(T.land[rank, 96:128, :], T.st[:, 7:8]).then_inc(S.packed, 16)
+    sc.wait_ge(S.aE2, 1)
+    sc.dma_start(T.land[rank, 64:96, :], T.st[:, 4:5]).then_inc(S.packed, 16)
+
+    def fan(slot):
+        tr = []
+        for j, d in enumerate(mates):
+            rid, pid = topo.addr(d, core)
+            tr.append(RemoteDMATransfer(dst_ids=[DstId(rid=rid, pnc=pid)], dma_engine_mask=eng[j],
+                                        remote_sem=S.arrived, src=T.land[slot], dst=T.land[slot]))
+        g.remote_dma_fused(tr, local_sem=S.sent)
+
+    g.wait_ge(S.packed, 64)
+    rid, pid = topo.addr(peer, core)
+    g.remote_dma(T.land[rank], T.land[rank], S.peer_in, S.sent, pid, rid, eng[0])
+    fan(rank)
+    g.wait_ge(S.peer_in, 1)
+    fan(peer_rank)
+    g.wait_ge(S.sent, 1 + 2 * len(mates))
+
+    sy.wait_ge(S.packed, 64)
+    sy.wait_ge(S.peer_in, 1)
+    sy.wait_ge(S.arrived, 2 * len(mates))
+    sy.dma_start(T.gat[0:48, :], T.land[:]).then_inc(S.unp, 16)
+
+    te.wait_ge(S.selA, 1)
+    te.wait_ge(S.selB, 1)
+    te.wait_ge(S.selC, 1)
+    te.wait_ge(S.unp, 16)
+    te.matmul(T.fin[:, 0:24], T.gat[0:48, :], T.sel[0:48, 0:24], start=True, stop=True).then_inc(S.pf, 1)
+    te.matmul(T.fin2[:, 0:1], T.gat[0:48, :], T.sel[0:48, 48:49], start=True, stop=True).then_inc(S.pf2, 1)
+
+    ve.wait_ge(S.pf, 1)
+    ve.tensor_reduce(out=T.tl[:, 24:25], in_=T.fin[:, 0:12], axis=X, op=MIN).then_inc(S.t1, 1)
+    sc.wait_ge(S.t1, 1)
+    sc.activation(T.tl[:, 0:12], T.fin[:, 0:12], EXP, bias=T.tl[:, 24:25], scale=-1.0).then_inc(S.t2, 1)
+    ve.wait_ge(S.t1, 1)
+    ve.wait_ge(S.pf2, 1)
+    ve.tensor_scalar(T.tl[:, 25:26], T.tl[:, 24:25], -1.0, T.fin2[:, 0:1], MUL, SUB).then_inc(S.t3, 1)
+    ve.wait_ge(S.t2, 1)
+    ve.tensor_tensor(T.tl[:, 12:24], T.tl[:, 0:12], T.fin[:, 12:24], MUL).then_inc(S.t4, 1)
+    ve.wait_ge(S.t4, 1)
+    ve.tensor_reduce(out=T.tl[:, 26:27], in_=T.tl[:, 12:24], axis=X, op=ADD).then_inc(S.t5, 1)
+    sc.wait_ge(S.t5, 1)
+    sc.activation(T.tl[:, 27:28], T.tl[:, 26:27], LN).then_inc(S.t6, 1)
+    sc.wait_ge(S.t6, 1)
+    sc.wait_ge(S.t3, 1)
+    sc.activation(T.tl[:, 28:29], T.tl[:, 27:28], IDENT, bias=T.tl[:, 25:26], scale=1.0).then_inc(S.t7, 1)
+    sc.wait_ge(S.t7, 1)
+    sc.dma_start(T.l[:], T.tl[:, 28:29]).then_inc(S.stored, 16)
+    sc.wait_ge(S.stored, 16)

@@ -2,8 +2,10 @@ from concourse.bass import DstId, RemoteDMATransfer
 from concourse.mybir import AluOpType, AxisListType, ActivationFunctionType
 
 N = 12
-W1 = 64
+W1 = 256
 W2 = 512 - W1
+NT = 64
+D = 8.75 / NT
 
 SCRATCH = {
     "hsb": ("sbuf", [128, 128], "bfloat16"),
@@ -15,7 +17,9 @@ SCRATCH = {
     "st": ("sbuf", [128, 8], "float32"),
     "sel": ("sbuf", [128, 52], "float32"),
     "gat": ("sbuf", [128, 128], "float32"),
-    "tl": ("sbuf", [128, 32], "float32"),
+    "thr": ("sbuf", [128, NT], "float32"),
+    "cm": ("sbuf", [128, NT], "float32"),
+    "tl": ("sbuf", [128, 36], "float32"),
     "land": ("dram", [N, 128, 4], "float32"),
     "zA1": ("psum", [128, 512], "float32"),
     "zA2": ("psum", [128, 512], "float32"),
@@ -24,15 +28,15 @@ SCRATCH = {
     "fin": ("psum", [128, 512], "float32"),
     "fin2": ("psum", [128, 512], "float32"),
 }
-SEMAPHORES = ["ld_h", "ld_w1", "ld_w2", "ld_oh", "c_ones", "c_sel", "selA", "selB", "selC",
+SEMAPHORES = ["ld_h", "ld_w1", "ld_w2", "ld_oh", "c_ones", "c_sel", "selA", "selB", "selC", "iot", "thr_ok",
               "mA1", "mA2", "mB", "vA", "vB", "vC", "vp0", "vp1", "vp2", "vp3", "mT", "vT",
               "aE1", "aE", "aE2", "vS", "packed", "peer_in", "arrived", "sent", "unp",
-              "pf", "pf2", "t1", "t2", "t3", "t4", "t5", "t6", "t7", "stored"]
+              "pf", "pf2", "t1", "t2", "t3", "t4", "t5", "n1", "n2", "n3", "n4", "n5", "n6", "n7", "n8", "stored"]
 
 ADD, MUL, SUB = AluOpType.add, AluOpType.mult, AluOpType.subtract
 MAX, MIN = AluOpType.max, AluOpType.min
 X = AxisListType.X
-EXP, LN, IDENT = ActivationFunctionType.Exp, ActivationFunctionType.Ln, ActivationFunctionType.Identity
+EXP = ActivationFunctionType.Exp
 
 
 def _engines(topo, src, dsts):
@@ -62,6 +66,9 @@ def rank_program(g, core, T, topo):
     sc.dma_start(T.wsb[:, W1:512], T.w[:, W1:512]).then_inc(S.ld_w2, 16)
     sy.dma_start(T.ohsb[:], T.oh[:]).then_inc(S.ld_oh, 16)
 
+    g.iota(T.thr[:, 0:NT], [[1, NT]], 0, 0, allow_small_or_imprecise_dtypes=True).then_inc(S.iot, 1)
+    sc.wait_ge(S.iot, 1)
+    sc.activation(T.thr[:, 0:NT], T.thr[:, 0:NT], EXP, bias=0.5 * D, scale=D).then_inc(S.thr_ok, 1)
     ve.memset(T.sel[0:48, 0:48], 1.0).then_inc(S.c_sel, 1)
     ve.memset(T.ones[:, 0:1], 1.0).then_inc(S.c_ones, 1)
     g.wait_ge(S.c_sel, 1)
@@ -148,22 +155,41 @@ def rank_program(g, core, T, topo):
     te.matmul(T.fin[:, 0:24], T.gat[0:48, :], T.sel[0:48, 0:24], start=True, stop=True).then_inc(S.pf, 1)
     te.matmul(T.fin2[:, 0:1], T.gat[0:48, :], T.sel[0:48, 48:49], start=True, stop=True).then_inc(S.pf2, 1)
 
+    tl = T.tl
+    negM, MT, Ssum = tl[:, 24:25], tl[:, 25:26], tl[:, 26:27]
+    y0, E0, a0, y1, E1, a1, lcol = (tl[:, 27:28], tl[:, 28:29], tl[:, 29:30], tl[:, 30:31], tl[:, 31:32],
+                                    tl[:, 32:33], tl[:, 34:35])
     ve.wait_ge(S.pf, 1)
-    ve.tensor_reduce(out=T.tl[:, 24:25], in_=T.fin[:, 0:12], axis=X, op=MIN).then_inc(S.t1, 1)
+    ve.tensor_reduce(out=negM, in_=T.fin[:, 0:12], axis=X, op=MIN).then_inc(S.t1, 1)
     sc.wait_ge(S.t1, 1)
-    sc.activation(T.tl[:, 0:12], T.fin[:, 0:12], EXP, bias=T.tl[:, 24:25], scale=-1.0).then_inc(S.t2, 1)
+    sc.activation(tl[:, 0:12], T.fin[:, 0:12], EXP, bias=negM, scale=-1.0).then_inc(S.t2, 1)
     ve.wait_ge(S.t1, 1)
     ve.wait_ge(S.pf2, 1)
-    ve.tensor_scalar(T.tl[:, 25:26], T.tl[:, 24:25], -1.0, T.fin2[:, 0:1], MUL, SUB).then_inc(S.t3, 1)
+    ve.tensor_scalar(MT, negM, -1.0, T.fin2[:, 0:1], MUL, SUB).then_inc(S.t3, 1)
     ve.wait_ge(S.t2, 1)
-    ve.tensor_tensor(T.tl[:, 12:24], T.tl[:, 0:12], T.fin[:, 12:24], MUL).then_inc(S.t4, 1)
+    ve.tensor_tensor(tl[:, 12:24], tl[:, 0:12], T.fin[:, 12:24], MUL).then_inc(S.t4, 1)
     ve.wait_ge(S.t4, 1)
-    ve.tensor_reduce(out=T.tl[:, 26:27], in_=T.tl[:, 12:24], axis=X, op=ADD).then_inc(S.t5, 1)
-    sc.wait_ge(S.t5, 1)
-    sc.activation(T.tl[:, 27:28], T.tl[:, 26:27], LN).then_inc(S.t6, 1)
-    sc.wait_ge(S.t6, 1)
-    sc.wait_ge(S.t3, 1)
-    sc.activation(T.tl[:, 28:29], T.tl[:, 27:28], IDENT, bias=T.tl[:, 25:26], scale=1.0).then_inc(S.t7, 1)
-    sc.wait_ge(S.t7, 1)
-    sc.dma_start(T.l[:], T.tl[:, 28:29]).then_inc(S.stored, 16)
-    sc.wait_ge(S.stored, 16)
+    ve.tensor_reduce(out=Ssum, in_=tl[:, 12:24], axis=X, op=ADD).then_inc(S.t5, 1)
+    ve.wait_ge(S.t5, 1)
+    ve.wait_ge(S.thr_ok, 1)
+    ve.tensor_scalar(T.cm[:, 0:NT], T.thr[:, 0:NT], Ssum, D, AluOpType.is_le, MUL).then_inc(S.n1, 1)
+    ve.wait_ge(S.n1, 1)
+    ve.tensor_reduce(out=y0, in_=T.cm[:, 0:NT], axis=X, op=ADD).then_inc(S.n2, 1)
+    sc.wait_ge(S.n2, 1)
+    sc.activation(E0, y0, EXP, scale=-1.0).then_inc(S.n3, 1)
+    ve.wait_ge(S.n2, 1)
+    ve.tensor_scalar(a0, y0, -1.0, None, ADD).then_inc(S.n4, 1)
+    ve.wait_ge(S.n3, 1)
+    ve.wait_ge(S.n4, 1)
+    ve.tensor_scalar(y1, E0, Ssum, a0, MUL, ADD).then_inc(S.n5, 1)
+    sc.wait_ge(S.n5, 1)
+    sc.activation(E1, y1, EXP, scale=-1.0).then_inc(S.n6, 1)
+    ve.wait_ge(S.n5, 1)
+    ve.wait_ge(S.t3, 1)
+    ve.tensor_scalar(a1, y1, -1.0, MT, ADD, ADD).then_inc(S.n7, 1)
+    ve.wait_ge(S.n6, 1)
+    ve.wait_ge(S.n7, 1)
+    ve.tensor_scalar(lcol, E1, Ssum, a1, MUL, ADD).then_inc(S.n8, 1)
+    sy.wait_ge(S.n8, 1)
+    sy.dma_start(T.l[:], lcol).then_inc(S.stored, 16)
+    sy.wait_ge(S.stored, 16)

@@ -1,3 +1,5 @@
+import math
+import numpy as np
 from concourse.bass import DstId, RemoteDMATransfer
 from concourse.mybir import AluOpType, AxisListType, ActivationFunctionType
 
@@ -5,7 +7,21 @@ N = 12
 W1 = 256
 W2 = 512 - W1
 NT = 64
-D = 8.75 / NT
+XTOP = 6200.0
+D = math.log(XTOP) / (NT - 1)
+C = D / (XTOP * (math.exp(D) - 1.0))
+
+
+def _centre():
+    s = np.exp(np.linspace(math.log(0.9999), math.log(6144.5), 40001))
+    acc = np.zeros_like(s)
+    for k in range(NT):
+        acc += np.maximum(1.0 - s * math.exp(-k * D), 0.0)
+    e = -D * acc + C * s - np.log(s)
+    return float(-(e.max() + e.min()) / 2.0)
+
+
+K0 = _centre()
 
 SCRATCH = {
     "hsb": ("sbuf", [128, 128], "bfloat16"),
@@ -15,35 +31,25 @@ SCRATCH = {
     "prod": ("sbuf", [128, 512], "float32"),
     "ones": ("sbuf", [128, 4], "float32"),
     "st": ("sbuf", [128, 8], "float32"),
-    "sel": ("sbuf", [128, 52], "float32"),
-    "gat": ("sbuf", [128, 128], "float32"),
+    "land": ("sbuf", [128, 4 * N], "float32"),
     "thr": ("sbuf", [128, NT], "float32"),
+    "ntab": ("sbuf", [128, NT], "float32"),
     "cm": ("sbuf", [128, NT], "float32"),
-    "tl": ("sbuf", [128, 36], "float32"),
-    "land": ("dram", [N, 128, 4], "float32"),
+    "tl": ("sbuf", [128, 48], "float32"),
     "zA1": ("psum", [128, 512], "float32"),
     "zA2": ("psum", [128, 512], "float32"),
     "zv": ("psum", [128, 512], "float32"),
     "tgp": ("psum", [128, 512], "float32"),
-    "fin": ("psum", [128, 512], "float32"),
-    "fin2": ("psum", [128, 512], "float32"),
 }
-SEMAPHORES = ["ld_h", "ld_w1", "ld_w2", "ld_oh", "c_ones", "c_sel", "selA", "selB", "selC", "iot", "thr_ok",
+SEMAPHORES = ["ld_h", "ld_w1", "ld_w2", "ld_oh", "c_ones", "iot", "thr_ok", "tab_ok",
               "mA1", "mA2", "mB", "vA", "vB", "vC", "vp0", "vp1", "vp2", "vp3", "mT", "vT",
-              "aE1", "aE", "aE2", "vS", "packed", "peer_in", "arrived", "sent", "unp",
-              "pf", "pf2", "t1", "t2", "t3", "t4", "t5", "n1", "n2", "n3", "n4", "n5", "n6", "n7", "n8", "stored"]
+              "aE1", "aE", "aE2", "vS", "arr1", "arr2", "sent",
+              "t1", "t2", "t3", "t4", "t5", "t6", "t7", "n1", "n2", "n3", "n4", "n5", "n8", "stored"]
 
 ADD, MUL, SUB = AluOpType.add, AluOpType.mult, AluOpType.subtract
 MAX, MIN = AluOpType.max, AluOpType.min
 X = AxisListType.X
-EXP = ActivationFunctionType.Exp
-
-
-def _engines(topo, src, dsts):
-    m = topo.mask(src, dsts[0])
-    for d in dsts[1:]:
-        m &= topo.mask(src, d)
-    return [1 << i for i in range(16) if (m >> i) & 1]
+EXP, RELU = ActivationFunctionType.Exp, ActivationFunctionType.Relu
 
 
 def rank_program(g, core, T, topo):
@@ -58,8 +64,14 @@ def rank_program(g, core, T, topo):
     mates = [c for c in others if topo.rack(topo.host(c)) == my_rack]
     peer = [c for c in others if topo.rack(topo.host(c)) != my_rack
             and topo.may_write(core, c) and topo.chip(c) == topo.chip(core)][0]
-    peer_rank = T.rank_of(peer)
-    eng = _engines(topo, core, mates + [peer])
+    mask = topo.mask(core, peer)
+    for d in mates:
+        mask &= topo.mask(core, d)
+    ne = sum((mask >> i) & 1 for i in range(16))
+    rr = sorted([rank] + [T.rank_of(c) for c in mates])
+    lo, hi = 4 * rr[0], 4 * rr[-1] + 4
+    c0 = 4 * rank
+    own = T.land[:, c0:c0 + 4]
 
     sc.dma_start(T.hsb[:], T.h[:]).then_inc(S.ld_h, 16)
     sy.dma_start(T.wsb[:, 0:W1], T.w[:, 0:W1]).then_inc(S.ld_w1, 16)
@@ -68,14 +80,8 @@ def rank_program(g, core, T, topo):
 
     g.iota(T.thr[:, 0:NT], [[1, NT]], 0, 0, allow_small_or_imprecise_dtypes=True).then_inc(S.iot, 1)
     sc.wait_ge(S.iot, 1)
-    sc.activation(T.thr[:, 0:NT], T.thr[:, 0:NT], EXP, bias=0.5 * D, scale=D).then_inc(S.thr_ok, 1)
-    ve.memset(T.sel[0:48, 0:48], 1.0).then_inc(S.c_sel, 1)
+    sc.activation(T.thr[:, 0:NT], T.thr[:, 0:NT], EXP, scale=-D).then_inc(S.thr_ok, 1)
     ve.memset(T.ones[:, 0:1], 1.0).then_inc(S.c_ones, 1)
-    g.wait_ge(S.c_sel, 1)
-    g.affine_select(T.sel[0:48, 0:48], T.sel[0:48, 0:48], [[-1, 4], [-4, 12]], AluOpType.is_equal, 0.0, 0, 1).then_inc(S.selA, 1)
-    ve.wait_ge(S.selA, 1)
-    ve.tensor_reduce(out=T.sel[0:48, 48:49], in_=T.sel[0:48, 36:48], axis=X, op=ADD).then_inc(S.selB, 1)
-    ve.tensor_tensor(T.sel[0:48, 12:24], T.sel[0:48, 12:24], T.sel[0:48, 24:36], ADD).then_inc(S.selC, 1)
 
     te.wait_ge(S.ld_h, 16)
     te.wait_ge(S.ld_w1, 16)
@@ -86,13 +92,14 @@ def rank_program(g, core, T, topo):
         te.matmul(T.zv[:, 128 * b:128 * b + 128], T.wsb[:, 128 * b:128 * b + 128], T.hsb[:],
                   start=True, stop=True).then_inc(S.mB, 1)
 
+    negm = T.land[:, c0:c0 + 1]
     ve.wait_ge(S.mA1, 1)
     ve.tensor_reduce(out=T.st[:, 0:1], in_=T.zA1[:, 0:W1], axis=X, op=MAX, negate=True).then_inc(S.vA, 1)
     ve.wait_ge(S.mA2, 1)
     ve.tensor_reduce(out=T.st[:, 1:2], in_=T.zA2[:, 0:W2], axis=X, op=MAX, negate=True).then_inc(S.vB, 1)
     ve.wait_ge(S.vA, 1)
     ve.wait_ge(S.vB, 1)
-    ve.tensor_tensor(T.st[:, 2:3], T.st[:, 0:1], T.st[:, 1:2], MIN).then_inc(S.vC, 1)
+    ve.tensor_tensor(negm, T.st[:, 0:1], T.st[:, 1:2], MIN).then_inc(S.vC, 1)
     ve.wait_ge(S.mB, 4)
     ve.wait_ge(S.ld_oh, 16)
     for b in range(4):
@@ -103,9 +110,9 @@ def rank_program(g, core, T, topo):
     sc.activation(T.junk[:, 0:W1], T.zA1[:, 0:W1], EXP, bias=T.st[:, 0:1], scale=1.0,
                   accum_out=T.st[:, 3:4]).then_inc(S.aE1, 1)
     sc.wait_ge(S.vC, 1)
-    sc.activation(T.st[:, 5:6], T.st[:, 0:1], EXP, bias=T.st[:, 2:3], scale=-1.0).then_inc(S.aE, 1)
-    sc.activation(T.junk[:, W1:512], T.zA2[:, 0:W2], EXP, bias=T.st[:, 2:3], scale=1.0,
-                  accum_out=T.st[:, 4:5]).then_inc(S.aE2, 1)
+    sc.activation(T.st[:, 5:6], T.st[:, 0:1], EXP, bias=negm, scale=-1.0).then_inc(S.aE, 1)
+    sc.activation(T.junk[:, W1:512], T.zA2[:, 0:W2], EXP, bias=negm, scale=1.0,
+                  accum_out=T.land[:, c0 + 2:c0 + 3]).then_inc(S.aE2, 1)
 
     te.wait_ge(S.c_ones, 1)
     for b in range(4):
@@ -114,82 +121,69 @@ def rank_program(g, core, T, topo):
                   start=(b == 0), stop=(b == 3)).then_inc(S.mT, 1)
     ve.wait_ge(S.aE1, 1)
     ve.wait_ge(S.aE, 1)
-    ve.tensor_tensor(T.st[:, 6:7], T.st[:, 3:4], T.st[:, 5:6], MUL).then_inc(S.vS, 1)
+    ve.tensor_tensor(T.land[:, c0 + 1:c0 + 2], T.st[:, 3:4], T.st[:, 5:6], MUL).then_inc(S.vS, 1)
     ve.wait_ge(S.mT, 4)
-    ve.tensor_copy(T.st[:, 7:8], T.tgp[:, 0:1]).then_inc(S.vT, 1)
+    ve.tensor_copy(T.land[:, c0 + 3:c0 + 4], T.tgp[:, 0:1]).then_inc(S.vT, 1)
+    ve.wait_ge(S.thr_ok, 1)
+    ve.tensor_scalar(T.ntab[:, 0:NT], T.thr[:, 0:NT], -1.0, None, MUL).then_inc(S.tab_ok, 1)
 
-    sy.wait_ge(S.vC, 1)
-    sy.dma_start(T.land[rank, 0:32, :], T.st[:, 2:3]).then_inc(S.packed, 16)
-    sy.wait_ge(S.vS, 1)
-    sy.dma_start(T.land[rank, 32:64, :], T.st[:, 6:7]).then_inc(S.packed, 16)
-    sy.wait_ge(S.vT, 1)
-    sy.dma_start(T.land[rank, 96:128, :], T.st[:, 7:8]).then_inc(S.packed, 16)
-    sc.wait_ge(S.aE2, 1)
-    sc.dma_start(T.land[rank, 64:96, :], T.st[:, 4:5]).then_inc(S.packed, 16)
-
-    def fan(slot):
-        tr = []
-        for j, d in enumerate(mates):
-            rid, pid = topo.addr(d, core)
-            tr.append(RemoteDMATransfer(dst_ids=[DstId(rid=rid, pnc=pid)], dma_engine_mask=eng[j],
-                                        remote_sem=S.arrived, src=T.land[slot], dst=T.land[slot]))
-        g.remote_dma_fused(tr, local_sem=S.sent)
-
-    g.wait_ge(S.packed, 64)
+    g.wait_ge(S.vC, 1)
+    g.wait_ge(S.vS, 1)
+    g.wait_ge(S.vT, 1)
+    g.wait_ge(S.aE2, 1)
+    ids = []
+    for d in mates:
+        rid, pid = topo.addr(d, core)
+        ids.append(DstId(rid=rid, pnc=pid))
+    g.remote_dma_fused([RemoteDMATransfer(dst_ids=ids, dma_engine_mask=mask, remote_sem=S.arr1,
+                                          srcs=[own], dsts=[own for _ in mates])], local_sem=S.sent)
+    g.wait_ge(S.arr1, ne * len(mates))
     rid, pid = topo.addr(peer, core)
-    g.remote_dma(T.land[rank], T.land[rank], S.peer_in, S.sent, pid, rid, eng[0])
-    fan(rank)
-    g.wait_ge(S.peer_in, 1)
-    fan(peer_rank)
-    g.wait_ge(S.sent, 1 + 2 * len(mates))
-
-    sy.wait_ge(S.packed, 64)
-    sy.wait_ge(S.peer_in, 1)
-    sy.wait_ge(S.arrived, 2 * len(mates))
-    sy.dma_start(T.gat[0:48, :], T.land[:]).then_inc(S.unp, 16)
-
-    te.wait_ge(S.selA, 1)
-    te.wait_ge(S.selB, 1)
-    te.wait_ge(S.selC, 1)
-    te.wait_ge(S.unp, 16)
-    te.matmul(T.fin[:, 0:24], T.gat[0:48, :], T.sel[0:48, 0:24], start=True, stop=True).then_inc(S.pf, 1)
-    te.matmul(T.fin2[:, 0:1], T.gat[0:48, :], T.sel[0:48, 48:49], start=True, stop=True).then_inc(S.pf2, 1)
+    g.remote_dma(T.land[:, lo:hi], T.land[:, lo:hi], S.arr2, S.sent, pid, rid, mask)
+    g.wait_ge(S.sent, 2 * ne)
 
     tl = T.tl
-    negM, MT, Ssum = tl[:, 24:25], tl[:, 25:26], tl[:, 26:27]
-    y0, E0, a0, y1, E1, a1, lcol = (tl[:, 27:28], tl[:, 28:29], tl[:, 29:30], tl[:, 30:31], tl[:, 31:32],
-                                    tl[:, 32:33], tl[:, 34:35])
-    ve.wait_ge(S.pf, 1)
-    ve.tensor_reduce(out=negM, in_=T.fin[:, 0:12], axis=X, op=MIN).then_inc(S.t1, 1)
+    negM, U, Ssum, Tsum = tl[:, 24:25], tl[:, 25:26], tl[:, 26:27], tl[:, 27:28]
+    acc, nb, E0, b2, a, lcol = tl[:, 28:29], tl[:, 29:30], tl[:, 30:31], tl[:, 31:32], tl[:, 32:33], tl[:, 33:34]
+    mcols, s1cols, s2cols, tcols = T.land[:, 0::4], T.land[:, 1::4], T.land[:, 2::4], T.land[:, 3::4]
+    ve.wait_ge(S.vC, 1)
+    ve.wait_ge(S.vS, 1)
+    ve.wait_ge(S.vT, 1)
+    ve.wait_ge(S.aE2, 1)
+    ve.wait_ge(S.arr1, ne * len(mates))
+    ve.wait_ge(S.arr2, ne)
+    ve.tensor_reduce(out=negM, in_=mcols, axis=X, op=MIN).then_inc(S.t1, 1)
+    sc.wait_ge(S.arr1, ne * len(mates))
+    sc.wait_ge(S.arr2, ne)
     sc.wait_ge(S.t1, 1)
-    sc.activation(tl[:, 0:12], T.fin[:, 0:12], EXP, bias=negM, scale=-1.0).then_inc(S.t2, 1)
+    sc.activation(tl[:, 0:12], mcols, EXP, bias=negM, scale=-1.0).then_inc(S.t2, 1)
+    ve.tensor_tensor(tl[:, 36:48], s1cols, s2cols, ADD).then_inc(S.t6, 1)
+    ve.tensor_reduce(out=Tsum, in_=tcols, axis=X, op=ADD).then_inc(S.t7, 1)
     ve.wait_ge(S.t1, 1)
-    ve.wait_ge(S.pf2, 1)
-    ve.tensor_scalar(MT, negM, -1.0, T.fin2[:, 0:1], MUL, SUB).then_inc(S.t3, 1)
+    ve.wait_ge(S.t7, 1)
+    ve.tensor_scalar(U, Tsum, negM, 1.0, ADD, ADD).then_inc(S.t3, 1)
     ve.wait_ge(S.t2, 1)
-    ve.tensor_tensor(tl[:, 12:24], tl[:, 0:12], T.fin[:, 12:24], MUL).then_inc(S.t4, 1)
+    ve.wait_ge(S.t6, 1)
+    ve.tensor_tensor(tl[:, 12:24], tl[:, 0:12], tl[:, 36:48], MUL).then_inc(S.t4, 1)
     ve.wait_ge(S.t4, 1)
     ve.tensor_reduce(out=Ssum, in_=tl[:, 12:24], axis=X, op=ADD).then_inc(S.t5, 1)
+    sc.wait_ge(S.t5, 1)
+    sc.wait_ge(S.tab_ok, 1)
+    sc.activation(T.cm[:, 0:NT], T.ntab[:, 0:NT], RELU, bias=1.0, scale=Ssum, accum_out=acc).then_inc(S.n1, 1)
     ve.wait_ge(S.t5, 1)
-    ve.wait_ge(S.thr_ok, 1)
-    ve.tensor_scalar(T.cm[:, 0:NT], T.thr[:, 0:NT], Ssum, D, AluOpType.is_le, MUL).then_inc(S.n1, 1)
-    ve.wait_ge(S.n1, 1)
-    ve.tensor_reduce(out=y0, in_=T.cm[:, 0:NT], axis=X, op=ADD).then_inc(S.n2, 1)
+    ve.tensor_scalar(nb, Ssum, -C, -K0, MUL, ADD).then_inc(S.n2, 1)
+    sc.wait_ge(S.n1, 1)
     sc.wait_ge(S.n2, 1)
-    sc.activation(E0, y0, EXP, scale=-1.0).then_inc(S.n3, 1)
+    sc.activation(E0, acc, EXP, bias=nb, scale=D).then_inc(S.n3, 1)
     ve.wait_ge(S.n2, 1)
-    ve.tensor_scalar(a0, y0, -1.0, None, ADD).then_inc(S.n4, 1)
-    ve.wait_ge(S.n3, 1)
-    ve.wait_ge(S.n4, 1)
-    ve.tensor_scalar(y1, E0, Ssum, a0, MUL, ADD).then_inc(S.n5, 1)
-    sc.wait_ge(S.n5, 1)
-    sc.activation(E1, y1, EXP, scale=-1.0).then_inc(S.n6, 1)
-    ve.wait_ge(S.n5, 1)
     ve.wait_ge(S.t3, 1)
-    ve.tensor_scalar(a1, y1, -1.0, MT, ADD, ADD).then_inc(S.n7, 1)
-    ve.wait_ge(S.n6, 1)
-    ve.wait_ge(S.n7, 1)
-    ve.tensor_scalar(lcol, E1, Ssum, a1, MUL, ADD).then_inc(S.n8, 1)
+    ve.tensor_scalar(b2, nb, U, -1.0, ADD, MUL).then_inc(S.n4, 1)
+    ve.wait_ge(S.n1, 1)
+    ve.wait_ge(S.n4, 1)
+    ve.tensor_scalar(a, acc, -D, b2, MUL, ADD).then_inc(S.n5, 1)
+    ve.wait_ge(S.n3, 1)
+    ve.wait_ge(S.n5, 1)
+    ve.tensor_scalar(lcol, E0, Ssum, a, MUL, ADD).then_inc(S.n8, 1)
     sy.wait_ge(S.n8, 1)
     sy.dma_start(T.l[:], lcol).then_inc(S.stored, 16)
     sy.wait_ge(S.stored, 16)

import math
import numpy as np
from concourse.bass import DstId, RemoteDMATransfer
from concourse.mybir import AluOpType, AxisListType, ActivationFunctionType

N = 12
W1 = 256
W2 = 512 - W1
NT = 64
XTOP = 6200.0
D = math.log(XTOP) / (NT - 1)
C = D / (XTOP * (math.exp(D) - 1.0))


def _centre():
    s = np.exp(np.linspace(math.log(0.9999), math.log(6144.5), 40001))
    acc = np.zeros_like(s)
    for k in range(NT):
        acc += np.maximum(1.0 - s * math.exp(-k * D), 0.0)
    e = -D * acc + C * s - np.log(s)
    return float(-(e.max() + e.min()) / 2.0)


K0 = _centre()

SCRATCH = {
    "hsb": ("sbuf", [128, 128], "bfloat16"),
    "wsb": ("sbuf", [128, 512], "bfloat16"),
    "ohsb": ("sbuf", [128, 512], "bfloat16"),
    "junk": ("sbuf", [128, 512], "float32"),
    "prod": ("sbuf", [128, 512], "float32"),
    "ones": ("sbuf", [128, 4], "float32"),
    "st": ("sbuf", [128, 8], "float32"),
    "land": ("sbuf", [128, 4 * N], "float32"),
    "thr": ("sbuf", [128, NT], "float32"),
    "ntab": ("sbuf", [128, NT], "float32"),
    "cm": ("sbuf", [128, NT], "float32"),
    "tl": ("sbuf", [128, 48], "float32"),
    "zA1": ("psum", [128, 512], "float32"),
    "zA2": ("psum", [128, 512], "float32"),
    "zv": ("psum", [128, 512], "float32"),
    "tgp": ("psum", [128, 512], "float32"),
}
SEMAPHORES = ["ld_h", "ld_w1", "ld_w2", "ld_oh", "c_ones", "iot", "thr_ok", "tab_ok",
              "mA1", "mA2", "mB", "vA", "vB", "vC", "vp0", "vp1", "vp2", "vp3", "mT", "vT",
              "aE1", "aE", "aE2", "vS", "arr1", "arr2", "sent",
              "t1", "t2", "t3", "t4", "t5", "t6", "t7", "n1", "n2", "n3", "n4", "n5", "n8", "stored"]

ADD, MUL, SUB = AluOpType.add, AluOpType.mult, AluOpType.subtract
MAX, MIN = AluOpType.max, AluOpType.min
X = AxisListType.X
EXP, RELU = ActivationFunctionType.Exp, ActivationFunctionType.Relu


def rank_program(g, core, T, topo):
    rank = T.rank_of(core)
    if rank is None:
        return
    S = T.sem
    te, ve, sc, sy = g.tensor, g.vector, g.scalar, g.sync

    my_rack = topo.rack(topo.host(core))
    others = [c for c in T.cores if c != core]
    mates = [c for c in others if topo.rack(topo.host(c)) == my_rack]
    peer = [c for c in others if topo.rack(topo.host(c)) != my_rack
            and topo.may_write(core, c) and topo.chip(c) == topo.chip(core)][0]
    mask = topo.mask(core, peer)
    for d in mates:
        mask &= topo.mask(core, d)
    ne = sum((mask >> i) & 1 for i in range(16))
    rr = sorted([rank] + [T.rank_of(c) for c in mates])
    lo, hi = 4 * rr[0], 4 * rr[-1] + 4
    c0 = 4 * rank
    own = T.land[:, c0:c0 + 4]

    sc.dma_start(T.hsb[:], T.h[:]).then_inc(S.ld_h, 16)
    sy.dma_start(T.wsb[:, 0:W1], T.w[:, 0:W1]).then_inc(S.ld_w1, 16)
    sc.dma_start(T.wsb[:, W1:512], T.w[:, W1:512]).then_inc(S.ld_w2, 16)
    sy.dma_start(T.ohsb[:], T.oh[:]).then_inc(S.ld_oh, 16)

    g.iota(T.thr[:, 0:NT], [[1, NT]], 0, 0, allow_small_or_imprecise_dtypes=True).then_inc(S.iot, 1)
    sc.wait_ge(S.iot, 1)
    sc.activation(T.thr[:, 0:NT], T.thr[:, 0:NT], EXP, scale=-D).then_inc(S.thr_ok, 1)
    ve.memset(T.ones[:, 0:1], 1.0).then_inc(S.c_ones, 1)

    te.wait_ge(S.ld_h, 16)
    te.wait_ge(S.ld_w1, 16)
    te.matmul(T.zA1[:, 0:W1], T.hsb[:], T.wsb[:, 0:W1], start=True, stop=True).then_inc(S.mA1, 1)
    te.wait_ge(S.ld_w2, 16)
    te.matmul(T.zA2[:, 0:W2], T.hsb[:], T.wsb[:, W1:512], start=True, stop=True).then_inc(S.mA2, 1)
    for b in range(4):
        te.matmul(T.zv[:, 128 * b:128 * b + 128], T.wsb[:, 128 * b:128 * b + 128], T.hsb[:],
                  start=True, stop=True).then_inc(S.mB, 1)

    negm = T.land[:, c0:c0 + 1]
    ve.wait_ge(S.mA1, 1)
    ve.tensor_reduce(out=T.st[:, 0:1], in_=T.zA1[:, 0:W1], axis=X, op=MAX, negate=True).then_inc(S.vA, 1)
    ve.wait_ge(S.mA2, 1)
    ve.tensor_reduce(out=T.st[:, 1:2], in_=T.zA2[:, 0:W2], axis=X, op=MAX, negate=True).then_inc(S.vB, 1)
    ve.wait_ge(S.vA, 1)
    ve.wait_ge(S.vB, 1)
    ve.tensor_tensor(negm, T.st[:, 0:1], T.st[:, 1:2], MIN).then_inc(S.vC, 1)
    ve.wait_ge(S.mB, 4)
    ve.wait_ge(S.ld_oh, 16)
    for b in range(4):
        blk = slice(128 * b, 128 * b + 128)
        ve.tensor_tensor(T.prod[:, blk], T.zv[:, blk], T.ohsb[:, blk], MUL).then_inc(S["vp%d" % b], 1)

    sc.wait_ge(S.vA, 1)
    sc.activation(T.junk[:, 0:W1], T.zA1[:, 0:W1], EXP, bias=T.st[:, 0:1], scale=1.0,
                  accum_out=T.st[:, 3:4]).then_inc(S.aE1, 1)
    sc.wait_ge(S.vC, 1)
    sc.activation(T.st[:, 5:6], T.st[:, 0:1], EXP, bias=negm, scale=-1.0).then_inc(S.aE, 1)
    sc.activation(T.junk[:, W1:512], T.zA2[:, 0:W2], EXP, bias=negm, scale=1.0,
                  accum_out=T.land[:, c0 + 2:c0 + 3]).then_inc(S.aE2, 1)

    te.wait_ge(S.c_ones, 1)
    for b in range(4):
        te.wait_ge(S["vp%d" % b], 1)
        te.matmul(T.tgp[:, 0:1], T.prod[:, 128 * b:128 * b + 128], T.ones[:, 0:1],
                  start=(b == 0), stop=(b == 3)).then_inc(S.mT, 1)
    ve.wait_ge(S.aE1, 1)
    ve.wait_ge(S.aE, 1)
    ve.tensor_tensor(T.land[:, c0 + 1:c0 + 2], T.st[:, 3:4], T.st[:, 5:6], MUL).then_inc(S.vS, 1)
    ve.wait_ge(S.mT, 4)
    ve.tensor_copy(T.land[:, c0 + 3:c0 + 4], T.tgp[:, 0:1]).then_inc(S.vT, 1)
    ve.wait_ge(S.thr_ok, 1)
    ve.tensor_scalar(T.ntab[:, 0:NT], T.thr[:, 0:NT], -1.0, None, MUL).then_inc(S.tab_ok, 1)

    g.wait_ge(S.vC, 1)
    g.wait_ge(S.vS, 1)
    g.wait_ge(S.vT, 1)
    g.wait_ge(S.aE2, 1)
    ids = []
    for d in mates:
        rid, pid = topo.addr(d, core)
        ids.append(DstId(rid=rid, pnc=pid))
    g.remote_dma_fused([RemoteDMATransfer(dst_ids=ids, dma_engine_mask=mask, remote_sem=S.arr1,
                                          srcs=[own], dsts=[own for _ in mates])], local_sem=S.sent)
    g.wait_ge(S.arr1, ne * len(mates))
    rid, pid = topo.addr(peer, core)
    g.remote_dma(T.land[:, lo:hi], T.land[:, lo:hi], S.arr2, S.sent, pid, rid, mask)
    g.wait_ge(S.sent, 2 * ne)

    tl = T.tl
    negM, U, Ssum, Tsum = tl[:, 24:25], tl[:, 25:26], tl[:, 26:27], tl[:, 27:28]
    acc, nb, E0, b2, a, lcol = tl[:, 28:29], tl[:, 29:30], tl[:, 30:31], tl[:, 31:32], tl[:, 32:33], tl[:, 33:34]
    mcols, s1cols, s2cols, tcols = T.land[:, 0::4], T.land[:, 1::4], T.land[:, 2::4], T.land[:, 3::4]
    ve.wait_ge(S.vC, 1)
    ve.wait_ge(S.vS, 1)
    ve.wait_ge(S.vT, 1)
    ve.wait_ge(S.aE2, 1)
    ve.wait_ge(S.arr1, ne * len(mates))
    ve.wait_ge(S.arr2, ne)
    ve.tensor_reduce(out=negM, in_=mcols, axis=X, op=MIN).then_inc(S.t1, 1)
    sc.wait_ge(S.arr1, ne * len(mates))
    sc.wait_ge(S.arr2, ne)
    sc.wait_ge(S.t1, 1)
    sc.activation(tl[:, 0:12], mcols, EXP, bias=negM, scale=-1.0).then_inc(S.t2, 1)
    ve.tensor_tensor(tl[:, 36:48], s1cols, s2cols, ADD).then_inc(S.t6, 1)
    ve.tensor_reduce(out=Tsum, in_=tcols, axis=X, op=ADD).then_inc(S.t7, 1)
    ve.wait_ge(S.t1, 1)
    ve.wait_ge(S.t7, 1)
    ve.tensor_scalar(U, Tsum, negM, 1.0, ADD, ADD).then_inc(S.t3, 1)
    ve.wait_ge(S.t2, 1)
    ve.wait_ge(S.t6, 1)
    ve.tensor_tensor(tl[:, 12:24], tl[:, 0:12], tl[:, 36:48], MUL).then_inc(S.t4, 1)
    ve.wait_ge(S.t4, 1)
    ve.tensor_reduce(out=Ssum, in_=tl[:, 12:24], axis=X, op=ADD).then_inc(S.t5, 1)
    sc.wait_ge(S.t5, 1)
    sc.wait_ge(S.tab_ok, 1)
    sc.activation(T.cm[:, 0:NT], T.ntab[:, 0:NT], RELU, bias=1.0, scale=Ssum, accum_out=acc).then_inc(S.n1, 1)
    ve.wait_ge(S.t5, 1)
    ve.tensor_scalar(nb, Ssum, -C, -K0, MUL, ADD).then_inc(S.n2, 1)
    sc.wait_ge(S.n1, 1)
    sc.wait_ge(S.n2, 1)
    sc.activation(E0, acc, EXP, bias=nb, scale=D).then_inc(S.n3, 1)
    ve.wait_ge(S.n2, 1)
    ve.wait_ge(S.t3, 1)
    ve.tensor_scalar(b2, nb, U, -1.0, ADD, MUL).then_inc(S.n4, 1)
    ve.wait_ge(S.n1, 1)
    ve.wait_ge(S.n4, 1)
    ve.tensor_scalar(a, acc, -D, b2, MUL, ADD).then_inc(S.n5, 1)
    ve.wait_ge(S.n3, 1)
    ve.wait_ge(S.n5, 1)
    ve.tensor_scalar(lcol, E0, Ssum, a, MUL, ADD).then_inc(S.n8, 1)
    sy.wait_ge(S.n8, 1)
    sy.dma_start(T.l[:], lcol).then_inc(S.stored, 16)
    sy.wait_ge(S.stored, 16)
